import numpy as np
import ml_dtypes


def mxq(x, axis, fmt="e4m3"):
    dtype, down = {"e4m3": (ml_dtypes.float8_e4m3fn, 7), "e5m2": (ml_dtypes.float8_e5m2, 14)}[fmt]
    v = np.moveaxis(np.asarray(x, np.float32).astype(ml_dtypes.bfloat16).astype(np.float64), axis, -1)
    blocks = v.reshape(v.shape[:-1] + (-1, 32))
    amax = np.abs(blocks).max(-1, keepdims=True)
    byte = np.maximum(np.where(amax > 0, np.frexp(amax)[1] - 1 + 127, 0) - down, 1)
    scale = np.exp2(byte - 127.0)
    codes = (blocks / scale).astype(np.float32).astype(dtype).astype(np.float64)
    return np.moveaxis((codes * scale).reshape(v.shape), -1, axis)


WIDE = False


def mx_kscale(k):
    if not WIDE:
        return np.ones(k)
    levels = np.array([10, -10, 5, -5, 0])
    if k % 512:
        return np.exp2(np.random.permutation(np.resize(levels, k // 32))).repeat(32)
    a = np.empty((k // 512, 16))
    for p in range(k // 512):
        a[p, :8] = np.random.permutation(np.resize(levels, 8))
        for g in range(8):
            far = levels[np.abs(levels - a[p, g]) >= 10]
            a[p, g + 8] = far[np.random.randint(len(far))]
    return np.exp2(a.ravel()).repeat(32)


def f64(x):
    return np.asarray(x).astype(np.float64)


def striped(idx):
    return np.tile(idx.reshape(-1, 16).T, (8, 1)).astype(np.uint16)


def unstriped(offs):
    return offs[:16].T.reshape(-1).astype(np.int64)


def pack_weight(w):
    k, n = w.shape
    w = f64(np.asarray(w, np.float32).astype(ml_dtypes.bfloat16)).reshape(k // 32, 32, n)
    amax = np.abs(w).max(1)
    byte = np.clip(np.where(amax > 0, np.frexp(amax)[1] - 1 + 127 - 7, 1), 1, 254)
    scaled = (w * np.exp2(127.0 - byte)[:, None, :]).reshape(k, n).astype(np.float32)
    words = np.ascontiguousarray(scaled.reshape(k // 512, 128, 4, n).transpose(0, 1, 3, 2)).astype(ml_dtypes.float8_e4m3fn).view(np.uint8)
    return words, np.ascontiguousarray(byte.astype(np.uint8).reshape(k // 512, 16, n))


def unpack_weight(words, scales):
    g, p, n, _ = words.shape
    vals = np.ascontiguousarray(words).view(ml_dtypes.float8_e4m3fn).astype(np.float64) * np.repeat(np.exp2(scales.astype(np.float64) - 127.0), 8, axis=1)[..., None]
    return vals.transpose(0, 1, 3, 2).reshape(g * 512, n)


E2M1 = np.array([0.0, 0.5, 1.0, 1.5, 2.0, 3.0, 4.0, 6.0, -0.0, -0.5, -1.0, -1.5, -2.0, -3.0, -4.0, -6.0])


def pack_fp4(w):
    k, n = w.shape
    w = f64(np.asarray(w, np.float32).astype(ml_dtypes.bfloat16)).reshape(k // 32, 32, n)
    amax = np.abs(w).max(1)
    mant, ex = np.frexp(amax / 6.0)
    byte = np.clip(np.where(amax > 0, np.where(mant > 0.5, ex, ex - 1) + 127, 1), 1, 254)
    scaled = (w * np.exp2(127.0 - byte)[:, None, :]).reshape(k, n).astype(np.float32)
    c = np.ascontiguousarray(scaled.reshape(k // 512, 128, 4, n).transpose(0, 1, 3, 2)).astype(ml_dtypes.float4_e2m1fn).view(np.uint8) & 0xF
    words = (c[..., 0::2] | (c[..., 1::2] << 4)).reshape(k // 512, 128, 2 * n)
    return np.ascontiguousarray(words), np.ascontiguousarray(byte.astype(np.uint8).reshape(k // 512, 16, n))


def unpack_fp4(words, scales):
    g, _, n = scales.shape
    words = np.ascontiguousarray(words).reshape(g, 128, n, 2)
    nib = np.empty((g, 128, n, 4), np.uint8)
    nib[..., 0::2] = words & 0xF
    nib[..., 1::2] = words >> 4
    vals = E2M1[nib] * np.repeat(np.exp2(scales.astype(np.float64) - 127.0), 8, axis=1)[..., None]
    return vals.transpose(0, 1, 3, 2).reshape(g * 512, n)


K, T, S, N, H = 512, 2048, 512, 256, 512


def setup_inputs():
    n = np.random.standard_normal
    s = mx_kscale(K)[:, None]
    u = mx_kscale(H)
    packed_xT = pack_weight(n((K, T)) * s)
    packed_w1 = pack_fp4(n((K, H)) / np.sqrt(K) / s)
    packed_w2 = pack_fp4(n((K, H)) / np.sqrt(K) / s)
    packed_w3 = pack_fp4(n((H, N)) / np.sqrt(H) / u[:, None])
    return {
        "x_words": packed_xT[0],
        "x_scales": packed_xT[1],
        "w1_words": packed_w1[0],
        "w1_scales": packed_w1[1],
        "w2_words": packed_w2[0],
        "w2_scales": packed_w2[1],
        "f0": (np.random.uniform(0.8, 1.2, (H, S))).astype(np.float32),
        "dr": (np.random.uniform(0.3, 0.8, (H, 1))).astype(np.float32),
        "unit": (np.random.uniform(0.6, 1.4, (H, 1)) * u[:, None]).astype(np.float32),
        "w3_words": packed_w3[0],
        "w3_scales": packed_w3[1],
        "offs": striped(np.random.permutation(T)[:S]),
        "nb": striped(np.random.permutation(S)),
    }


def reference(x_words, x_scales, w1_words, w1_scales, w2_words, w2_scales, f0, dr, unit, w3_words, w3_scales, offs, nb):
    xq = unpack_weight(x_words, x_scales)[:, unstriped(offs)]
    vt = unpack_fp4(w2_words, w2_scales).T @ xq
    volt = 0.3 * np.tanh(vt) + 1.0
    vn = volt[:, unstriped(nb)]
    pw = unpack_fp4(w1_words, w1_scales).T @ xq
    freq = f64(f0) - (f64(dr) * np.tanh(pw))
    fn = freq[:, unstriped(nb)]
    slip = freq - fn
    flow = (volt * vn) * np.tanh(2.0 * slip)
    hid = f64(unit) * (flow * freq + volt)
    return unpack_fp4(w3_words, w3_scales).T @ mxq(hid, 0, "e4m3")

@@ -1,0 +1,186 @@
+from contextlib import ExitStack
+
+import concourse.mybir as mybir
+
+K, T, S, N, H = 512, 2048, 512, 256, 512
+FLOPS = 2 * K * H * S * 2 + 2 * H * N * S
+
+F32 = mybir.dt.float32
+BF16 = mybir.dt.bfloat16
+I32 = mybir.dt.int32
+U32 = mybir.dt.uint32
+U16 = mybir.dt.uint16
+U8 = mybir.dt.uint8
+FP8X4 = mybir.dt.float8_e4m3fn_x4
+FP4X4 = mybir.dt.float4_e2m1fn_x4
+ALU = mybir.AluOpType
+ACT = mybir.ActivationFunctionType
+
+P = 128
+PACK = 4
+HALF = S // 2
+CHUNKS = ((0, 256), (256, 384), (384, 512))
+
+
+def tile_picked_ydroopc_flow_p_kernel(tc, x_words, x_scales, w1_words, w1_scales, w2_words, w2_scales, f0, dr, unit, w3_words, w3_scales, offs, nb, out):
+    nc = tc.nc
+    with ExitStack() as ctx:
+        keep = ctx.enter_context(tc.tile_pool(name="keep", bufs=1))
+        psum = ctx.enter_context(tc.psum_pool(name="psum", bufs=1))
+
+        def load_scales(queues, plane, scales):
+            for q in range(4):
+                queues[q].dma_start(out=plane[32 * q : 32 * q + 4, :].bitcast(I32), in_=scales[0, 4 * q : 4 * q + 4, :].bitcast(I32))
+
+        def deal_words(name, words):
+            dw = keep.tile([P, PACK, 2 * P], U8, name=name, align_bytes=64)
+            nc.vector.tensor_copy(out=dw[:].rearrange("p t (m b) -> p t m b", b=2), in_=words[:].rearrange("p (m t b) -> p t m b", t=PACK, b=2))
+            return dw
+
+        def deal_plane(name, plane):
+            ds = keep.tile([P, PACK, P], U8, name=name, align_bytes=64)
+            nc.vector.tensor_copy(out=ds[:], in_=plane[:].rearrange("p (m t) -> p t m", t=PACK))
+            return ds
+
+        lap = ctx.enter_context(tc.tile_pool(name="lap", bufs=1))
+        offs_sb = keep.tile([P, S // 16], U16, name="offs_sb")
+        nb_sb = keep.tile([P, S // 16], U16, name="nb_sb")
+        xw = keep.tile([P, T], U32, name="xw", align_bytes=64)
+        xs = keep.tile([P, T], U8, name="xs", tag="ta", align_bytes=64)
+        w1w = lap.tile([P, 2 * H], U8, name="w1w", offset=8192 - 512, align_bytes=64)
+        w1s = keep.tile([P, H], U8, name="w1s", tag="tc", align_bytes=64)
+        dr_sb = keep.tile([P, PACK], F32, name="dr_sb")
+        unit_sb = keep.tile([P, PACK], F32, name="unit_sb")
+        xsg = keep.tile([P, S], U8, name="xsg", align_bytes=64)
+        xwg = keep.tile([P, S], U32, name="xwg", align_bytes=64)
+
+        nc.gpsimd.memset(xs[:].bitcast(I32), 0)
+        nc.gpsimd.memset(w1s[:].bitcast(I32), 0)
+
+        nc.sync.dma_start(offs_sb[:], offs)
+        nc.sync.dma_start(nb_sb[:], nb)
+        nc.sync.dma_start(out=w1w[:].bitcast(I32), in_=w1_words[0].bitcast(I32))
+        nc.sync.dma_start(out=xw[:].bitcast(I32), in_=x_words[0].rearrange("p n t -> p (n t)").bitcast(I32))
+        load_scales([nc.scalar] * 4, xs, x_scales)
+        load_scales([nc.scalar] * 3 + [nc.gpsimd], w1s, w1_scales)
+        nc.gpsimd.dma_start(out=dr_sb[:], in_=dr.rearrange("(p t) o -> p (t o)", t=PACK))
+        nc.gpsimd.dma_start(out=unit_sb[:], in_=unit.rearrange("(p t) o -> p (t o)", t=PACK))
+
+        d1w = deal_words("d1w", w1w)
+        nc.vector.tensor_copy(xsg[:], xs[:].indirect(offs_sb[:]))
+        d1s = deal_plane("d1s", w1s)
+        for c in range(2):
+            nc.vector.tensor_copy(xwg[:, c * HALF : (c + 1) * HALF], xw[:].indirect(offs_sb[:, c * HALF // 16 : (c + 1) * HALF // 16]))
+
+        f0_rows = f0.rearrange("(p t) j -> p t j", t=PACK)
+        f0_sb = lap.tile([P, PACK, S], F32, name="f0_sb", offset=0, align_bytes=64)
+        nc.sync.dma_start(out=f0_sb[:, 0, :], in_=f0_rows[:, 0, :])
+        w2w = lap.tile([P, 2 * H], U8, name="w2w", offset=8192, align_bytes=64)
+        nc.sync.dma_start(out=w2w[:].bitcast(I32), in_=w2_words[0].bitcast(I32))
+        for t in range(1, PACK):
+            nc.sync.dma_start(out=f0_sb[:, t, :], in_=f0_rows[:, t, :])
+        w2s = keep.tile([P, H], U8, name="w2s", tag="ta", align_bytes=64)
+        nc.gpsimd.memset(w2s[:].bitcast(I32), 0)
+        load_scales([nc.sync] * 4, w2s, w2_scales)
+        d2w = deal_words("d2w", w2w)
+        d2s = deal_plane("d2s", w2s)
+        w3w = lap.tile([P, 2 * N], U8, name="w3w", offset=8192, align_bytes=64)
+        w3s = keep.tile([P, N], U8, name="w3s", tag="tc", align_bytes=64)
+        nc.gpsimd.memset(w3s[:].bitcast(I32), 0)
+        nc.sync.dma_start(out=w3w[:].bitcast(I32), in_=w3_words[0].bitcast(I32))
+        load_scales([nc.sync] * 4, w3s, w3_scales)
+
+        def product(bank, dw, ds, t, cols):
+            acc = psum.tile([P, cols.stop - cols.start], F32, name="acc", tag="bank%d" % bank)
+            nc.tensor.matmul_mx(out=acc[:], lhsT=dw[:, t, :].bitcast(FP4X4), lhsT_scale=ds[:, t, :], rhs=xwg[:, cols].bitcast(FP8X4), rhs_scale=xsg[:, cols], start=True, stop=True)
+            return acc
+
+        neg_freq = [keep.tile([P, S], F32, name="neg_freq%d" % t) for t in range(PACK)]
+        volt = [keep.tile([P, S], F32, name="volt%d" % t) for t in range(PACK)]
+        hid = keep.tile([P, PACK, S], BF16, name="hid", align_bytes=64)
+        gn = keep.tile([P, PACK, S], F32, name="gn")
+        slip = keep.tile([P, PACK, S], F32, name="slip")
+        th = keep.tile([P, PACK, S], F32, name="th")
+        pf = keep.tile([P, PACK, S], F32, name="pf")
+        qq = keep.tile([P, PACK, S], F32, name="qq")
+        aa = keep.tile([P, PACK, S], F32, name="aa")
+        bb = keep.tile([P, PACK, S], F32, name="bb")
+        vn = keep.tile([P, PACK, S], F32, name="vn")
+        WHOLE = slice(0, S)
+
+        def entries(cols):
+            return nb_sb[:, cols.start // 16 : cols.stop // 16]
+
+        def pieces(cols):
+            return [cols] if cols.stop - cols.start < S else [slice(0, HALF), slice(HALF, S)]
+
+        def frequency(t, bank, cols):
+            pw = product(bank, d1w, d1s, t, cols)
+            nc.scalar.activation(bb[:, t, cols], pw[:], ACT.Tanh)
+            nc.vector.scalar_tensor_tensor(neg_freq[t][:, cols], bb[:, t, cols], dr_sb[:, t : t + 1], f0_sb[:, t, cols], ALU.mult, ALU.subtract)
+
+        def voltage(t, bank):
+            vt = product(bank, d2w, d2s, t, WHOLE)
+            nc.scalar.activation(aa[:, t, :], vt[:], ACT.Tanh)
+            if t < 0:
+                nc.vector.tensor_scalar(volt[t][:], aa[:, t, :], 0.3, 1.0, ALU.mult, ALU.add)
+            else:
+                nc.scalar.activation(volt[t][:], aa[:, t, :], ACT.Copy, bias=1.0, scale=0.3)
+
+        def fetch(dst, window, cols, on_scalar):
+            for part in pieces(cols):
+                if on_scalar:
+                    nc.scalar.activation(dst[:, part], window[:].indirect(entries(part)), ACT.Copy)
+                else:
+                    nc.vector.tensor_copy(dst[:, part], window[:].indirect(entries(part)))
+
+        def slips(t, cols):
+            fetch(gn[:, t, :], neg_freq[t], cols, t >= 1)
+            nc.vector.tensor_tensor(slip[:, t, cols], gn[:, t, cols], neg_freq[t][:, cols], ALU.subtract)
+            nc.scalar.activation(th[:, t, cols], slip[:, t, cols], ACT.Tanh, scale=-2.0)
+
+        def hidden(t, cols):
+            nc.vector.scalar_tensor_tensor(pf[:, t, cols], th[:, t, cols], unit_sb[:, t : t + 1], neg_freq[t][:, cols], ALU.mult, ALU.mult)
+            if t >= 3:
+                fetch(vn[:, t, :], volt[t], cols, True)
+                nc.vector.tensor_tensor(qq[:, t, cols], vn[:, t, cols], pf[:, t, cols], ALU.mult)
+            else:
+                for part in pieces(cols):
+                    nc.vector.tensor_tensor(qq[:, t, part], volt[t][:].indirect(entries(part)), pf[:, t, part], ALU.mult)
+            nc.vector.scalar_tensor_tensor(hid[:, t, cols], qq[:, t, cols], unit_sb[:, t : t + 1], volt[t][:, cols], ALU.add, ALU.mult)
+
+        def feeders(c, cols):
+            width = cols.stop - cols.start
+            woven = keep.tile([P, width, PACK], BF16, name="woven%d" % c, align_bytes=64)
+            codes = keep.tile([P, width], U32, name="codes%d" % c, align_bytes=64)
+            plane = keep.tile([P, width], U8, name="plane%d" % c, align_bytes=64)
+            weave = nc.scalar.copy if c < 1 else nc.vector.tensor_copy
+            weave(out=woven[:].rearrange("p (g i) t -> p g t i", i=4), in_=hid[:, :, cols].rearrange("p t (g i) -> p g t i", i=4))
+            nc.vector.quantize_mx(out=codes[:].bitcast(FP8X4), scales=plane[:], in_=woven[:].rearrange("p j t -> p (j t)"))
+            acc = psum.tile([P, 2, width], F32, name="oacc", tag="bank%d" % (c + 1))
+            for h in range(2):
+                nc.tensor.matmul_mx(out=acc[:, h, :], lhsT=w3w[:, 2 * P * h : 2 * P * (h + 1)].bitcast(FP4X4), lhsT_scale=w3s[:, P * h : P * (h + 1)], rhs=codes[:].bitcast(FP8X4), rhs_scale=plane[:], start=True, stop=True)
+            res = keep.tile([P, 2, width], F32, name="res%d" % c)
+            nc.scalar.copy(res[:], acc[:])
+            nc.sync.dma_start(out=out.rearrange("(h m) j -> m h j", h=2)[:, :, cols], in_=res[:])
+
+        frequency(0, 0, slice(0, HALF))
+        frequency(0, 1, slice(HALF, S))
+        frequency(1, 2, WHOLE)
+        frequency(2, 3, WHOLE)
+        slips(0, WHOLE)
+        voltage(0, 4)
+        slips(1, WHOLE)
+        frequency(3, 5, WHOLE)
+        voltage(1, 6)
+        hidden(0, WHOLE)
+        slips(2, WHOLE)
+        voltage(2, 7)
+        voltage(3, 0)
+        hidden(1, WHOLE)
+        for lo, hi in CHUNKS:
+            slips(3, slice(lo, hi))
+        for c, (lo, hi) in enumerate(CHUNKS):
+            for t in (2, 3):
+                hidden(t, slice(lo, hi))
+            feeders(c, slice(lo, hi))

@@ -49,22 +49,19 @@ def tile_picked_ydroopc_flow_p_kernel(tc, x_words, x_scales, w1_words, w1_scales
         xs = keep.tile([P, T], U8, name="xs", tag="ta", align_bytes=64)
         w1w = lap.tile([P, 2 * H], U8, name="w1w", offset=8192 - 512, align_bytes=64)
         w1s = keep.tile([P, H], U8, name="w1s", tag="tc", align_bytes=64)
-        dr_sb = keep.tile([P, PACK], F32, name="dr_sb")
-        unit_sb = keep.tile([P, PACK], F32, name="unit_sb")
         xsg = keep.tile([P, S], U8, name="xsg", align_bytes=64)
         xwg = keep.tile([P, S], U32, name="xwg", align_bytes=64)
 
-        nc.gpsimd.memset(xs[:].bitcast(I32), 0)
-        nc.gpsimd.memset(w1s[:].bitcast(I32), 0)
+        nc.vector.memset(w1s[:].bitcast(I32), 0)
 
         nc.sync.dma_start(offs_sb[:], offs)
+        for q in range(4):
+            rows = x_scales[0, 4 * q : 4 * q + 4, :].bitcast(I32)
+            (nc.sync if q < 2 else nc.scalar).dma_start(out=xs[32 * q : 32 * q + 32, :].bitcast(I32), in_=rows.unsqueeze(0).to_broadcast([8, 4, T // 4]))
+        nc.scalar.dma_start(out=w1w[:].bitcast(I32), in_=w1_words[0].bitcast(I32))
+        nc.scalar.dma_start(out=xw[:].bitcast(I32), in_=x_words[0].rearrange("p n t -> p (n t)").bitcast(I32))
         nc.sync.dma_start(nb_sb[:], nb)
-        nc.sync.dma_start(out=w1w[:].bitcast(I32), in_=w1_words[0].bitcast(I32))
-        nc.sync.dma_start(out=xw[:].bitcast(I32), in_=x_words[0].rearrange("p n t -> p (n t)").bitcast(I32))
-        load_scales([nc.scalar] * 4, xs, x_scales)
-        load_scales([nc.scalar] * 3 + [nc.gpsimd], w1s, w1_scales)
-        nc.gpsimd.dma_start(out=dr_sb[:], in_=dr.rearrange("(p t) o -> p (t o)", t=PACK))
-        nc.gpsimd.dma_start(out=unit_sb[:], in_=unit.rearrange("(p t) o -> p (t o)", t=PACK))
+        load_scales([nc.sync] * 4, w1s, w1_scales)
 
         d1w = deal_words("d1w", w1w)
         nc.vector.tensor_copy(xsg[:], xs[:].indirect(offs_sb[:]))
@@ -75,18 +72,20 @@ def tile_picked_ydroopc_flow_p_kernel(tc, x_words, x_scales, w1_words, w1_scales
         f0_rows = f0.rearrange("(p t) j -> p t j", t=PACK)
         f0_sb = lap.tile([P, PACK, S], F32, name="f0_sb", offset=0, align_bytes=64)
         nc.sync.dma_start(out=f0_sb[:, 0, :], in_=f0_rows[:, 0, :])
-        w2w = lap.tile([P, 2 * H], U8, name="w2w", offset=8192, align_bytes=64)
+        dr_sb = lap.tile([P, PACK], F32, name="dr_sb", offset=8192, align_bytes=64)
+        unit_sb = lap.tile([P, PACK], F32, name="unit_sb", offset=8256, align_bytes=64)
+        nc.sync.dma_start(out=dr_sb[:], in_=dr.rearrange("(p t) o -> p (t o)", t=PACK))
+        w2w = lap.tile([P, 2 * H], U8, name="w2w", offset=8320, align_bytes=64)
         nc.sync.dma_start(out=w2w[:].bitcast(I32), in_=w2_words[0].bitcast(I32))
         for t in range(1, PACK):
             nc.sync.dma_start(out=f0_sb[:, t, :], in_=f0_rows[:, t, :])
-        w2s = keep.tile([P, H], U8, name="w2s", tag="ta", align_bytes=64)
-        nc.gpsimd.memset(w2s[:].bitcast(I32), 0)
+        nc.sync.dma_start(out=unit_sb[:], in_=unit.rearrange("(p t) o -> p (t o)", t=PACK))
+        w2s = w1s
         load_scales([nc.sync] * 4, w2s, w2_scales)
         d2w = deal_words("d2w", w2w)
         d2s = deal_plane("d2s", w2s)
-        w3w = lap.tile([P, 2 * N], U8, name="w3w", offset=8192, align_bytes=64)
-        w3s = keep.tile([P, N], U8, name="w3s", tag="tc", align_bytes=64)
-        nc.gpsimd.memset(w3s[:].bitcast(I32), 0)
+        w3w = lap.tile([P, 2 * N], U8, name="w3w", offset=8320, align_bytes=64)
+        w3s = w1s[:, 0:N]
         nc.sync.dma_start(out=w3w[:].bitcast(I32), in_=w3_words[0].bitcast(I32))
         load_scales([nc.sync] * 4, w3s, w3_scales)
 
@@ -122,7 +121,7 @@ def tile_picked_ydroopc_flow_p_kernel(tc, x_words, x_scales, w1_words, w1_scales
         def voltage(t, bank):
             vt = product(bank, d2w, d2s, t, WHOLE)
             nc.scalar.activation(aa[:, t, :], vt[:], ACT.Tanh)
-            if t < 0:
+            if t < 2:
                 nc.vector.tensor_scalar(volt[t][:], aa[:, t, :], 0.3, 1.0, ALU.mult, ALU.add)
             else:
                 nc.scalar.activation(volt[t][:], aa[:, t, :], ACT.Copy, bias=1.0, scale=0.3)
@@ -141,7 +140,7 @@ def tile_picked_ydroopc_flow_p_kernel(tc, x_words, x_scales, w1_words, w1_scales
 
         def hidden(t, cols):
             nc.vector.scalar_tensor_tensor(pf[:, t, cols], th[:, t, cols], unit_sb[:, t : t + 1], neg_freq[t][:, cols], ALU.mult, ALU.mult)
-            if t >= 3:
+            if t >= 2:
                 fetch(vn[:, t, :], volt[t], cols, True)
                 nc.vector.tensor_tensor(qq[:, t, cols], vn[:, t, cols], pf[:, t, cols], ALU.mult)
             else:
@@ -166,20 +165,13 @@ def tile_picked_ydroopc_flow_p_kernel(tc, x_words, x_scales, w1_words, w1_scales
 
         frequency(0, 0, slice(0, HALF))
         frequency(0, 1, slice(HALF, S))
-        frequency(1, 2, WHOLE)
-        frequency(2, 3, WHOLE)
-        slips(0, WHOLE)
-        voltage(0, 4)
-        slips(1, WHOLE)
-        frequency(3, 5, WHOLE)
-        voltage(1, 6)
+        for t in range(1, PACK):
+            frequency(t, t + 1, WHOLE)
+        for t in range(PACK):
+            slips(t, WHOLE)
+            voltage(t, (5 + t) % 8)
         hidden(0, WHOLE)
-        slips(2, WHOLE)
-        voltage(2, 7)
-        voltage(3, 0)
         hidden(1, WHOLE)
-        for lo, hi in CHUNKS:
-            slips(3, slice(lo, hi))
         for c, (lo, hi) in enumerate(CHUNKS):
             for t in (2, 3):
                 hidden(t, slice(lo, hi))

@@ -17,9 +17,31 @@ ALU = mybir.AluOpType
 ACT = mybir.ActivationFunctionType
 
 P = 128
-PACK = 4
+SLOTS = 4
+QUADS = 4
+QUAD = P // QUADS
+LIVE = 4
+PER_COLUMN = 16
+BANKS = 8
 HALF = S // 2
-CHUNKS = ((0, 256), (256, 384), (384, 512))
+WHOLE = slice(0, S)
+HALVES = (slice(0, HALF), slice(HALF, S))
+
+CHUNKS = (slice(0, 256), slice(256, 384), slice(384, 512))
+WEAVE_RUN = 4
+
+FREQ_GATHERS_ON_VECTOR = 1
+VOLTS_ON_VECTOR = 2
+VOLT_GATHERS_ON_VECTOR = 2
+WEAVES_ON_SCALAR = 1
+
+F0_AT = 0
+DR_AT = F0_AT + SLOTS * S * 4
+UNIT_AT = DR_AT + 64
+LATE_PLANE_AT = UNIT_AT + 64
+W2_WORDS_AT = LATE_PLANE_AT + H
+W1_WORDS_AT = DR_AT - 64
+W1_PLANE_AT = 10240
 
 
 def tile_picked_ydroopc_flow_p_kernel(tc, x_words, x_scales, w1_words, w1_scales, w2_words, w2_scales, f0, dr, unit, w3_words, w3_scales, offs, nb, out):
@@ -27,152 +49,157 @@ def tile_picked_ydroopc_flow_p_kernel(tc, x_words, x_scales, w1_words, w1_scales
     with ExitStack() as ctx:
         keep = ctx.enter_context(tc.tile_pool(name="keep", bufs=1))
         psum = ctx.enter_context(tc.psum_pool(name="psum", bufs=1))
+        reused = ctx.enter_context(tc.tile_pool(name="reused", bufs=1))
 
-        def load_scales(queues, plane, scales):
-            for q in range(4):
-                queues[q].dma_start(out=plane[32 * q : 32 * q + 4, :].bitcast(I32), in_=scales[0, 4 * q : 4 * q + 4, :].bitcast(I32))
+        def load_live_rows(plane, scales):
+            for q in range(QUADS):
+                nc.sync.dma_start(out=plane[QUAD * q : QUAD * q + LIVE, :].bitcast(I32), in_=scales[0, LIVE * q : LIVE * (q + 1), :].bitcast(I32))
 
         def deal_words(name, words):
-            dw = keep.tile([P, PACK, 2 * P], U8, name=name, align_bytes=64)
-            nc.vector.tensor_copy(out=dw[:].rearrange("p t (m b) -> p t m b", b=2), in_=words[:].rearrange("p (m t b) -> p t m b", t=PACK, b=2))
-            return dw
+            dealt = keep.tile([P, SLOTS, 2 * P], U8, name=name, align_bytes=64)
+            nc.vector.tensor_copy(out=dealt[:].rearrange("p t (m b) -> p t m b", b=2), in_=words[:].rearrange("p (m t b) -> p t m b", t=SLOTS, b=2))
+            return dealt
 
         def deal_plane(name, plane):
-            ds = keep.tile([P, PACK, P], U8, name=name, align_bytes=64)
-            nc.vector.tensor_copy(out=ds[:], in_=plane[:].rearrange("p (m t) -> p t m", t=PACK))
-            return ds
+            dealt = keep.tile([P, SLOTS, P], U8, name=name, align_bytes=64)
+            nc.vector.tensor_copy(out=dealt[:], in_=plane[:].rearrange("p (m t) -> p t m", t=SLOTS))
+            return dealt
 
-        lap = ctx.enter_context(tc.tile_pool(name="lap", bufs=1))
-        offs_sb = keep.tile([P, S // 16], U16, name="offs_sb")
-        nb_sb = keep.tile([P, S // 16], U16, name="nb_sb")
-        xw = keep.tile([P, T], U32, name="xw", align_bytes=64)
-        xs = keep.tile([P, T], U8, name="xs", tag="ta", align_bytes=64)
-        w1w = lap.tile([P, 2 * H], U8, name="w1w", offset=8192 - 512, align_bytes=64)
-        w1s = keep.tile([P, H], U8, name="w1s", tag="tc", align_bytes=64)
-        xsg = keep.tile([P, S], U8, name="xsg", align_bytes=64)
-        xwg = keep.tile([P, S], U32, name="xwg", align_bytes=64)
+        def entries(list_sb, cols):
+            return list_sb[:, cols.start // PER_COLUMN : cols.stop // PER_COLUMN]
 
-        nc.vector.memset(w1s[:].bitcast(I32), 0)
+        offs_sb = keep.tile([P, S // PER_COLUMN], U16, name="offs_sb")
+        nb_sb = keep.tile([P, S // PER_COLUMN], U16, name="nb_sb")
+        x_table = keep.tile([P, T], U32, name="x_table", align_bytes=64)
+        x_table_plane = keep.tile([P, T], U8, name="x_table_plane", align_bytes=64)
+        w1_raw = reused.tile([P, 2 * H], U8, name="w1_raw", offset=W1_WORDS_AT, align_bytes=64)
+        w1_raw_plane = reused.tile([P, H], U8, name="w1_raw_plane", offset=W1_PLANE_AT, align_bytes=64)
+        x_plane = keep.tile([P, S], U8, name="x_plane", align_bytes=64)
+        x_picked = [
+            keep.tile([P, HALF], U32, name="x_picked0", align_bytes=64),
+            reused.tile([P, HALF], U32, name="x_picked1", offset=W1_PLANE_AT, align_bytes=64),
+        ]
+
+        nc.vector.memset(w1_raw_plane[:].bitcast(I32), 0)
 
         nc.sync.dma_start(offs_sb[:], offs)
-        for q in range(4):
-            rows = x_scales[0, 4 * q : 4 * q + 4, :].bitcast(I32)
-            (nc.sync if q < 2 else nc.scalar).dma_start(out=xs[32 * q : 32 * q + 32, :].bitcast(I32), in_=rows.unsqueeze(0).to_broadcast([8, 4, T // 4]))
-        nc.scalar.dma_start(out=w1w[:].bitcast(I32), in_=w1_words[0].bitcast(I32))
-        nc.scalar.dma_start(out=xw[:].bitcast(I32), in_=x_words[0].rearrange("p n t -> p (n t)").bitcast(I32))
+        nc.scalar.dma_start(out=w1_raw[:].bitcast(I32), in_=w1_words[0].bitcast(I32))
+        for q in range(QUADS):
+            rows = x_scales[0, LIVE * q : LIVE * (q + 1), :].bitcast(I32)
+            queue = nc.sync if q < QUADS // 2 else nc.scalar
+            queue.dma_start(out=x_table_plane[QUAD * q : QUAD * (q + 1), :].bitcast(I32), in_=rows.unsqueeze(0).to_broadcast([QUAD // LIVE, LIVE, T // 4]))
+        nc.scalar.dma_start(out=x_table[:].bitcast(I32), in_=x_words[0].rearrange("p n t -> p (n t)").bitcast(I32))
         nc.sync.dma_start(nb_sb[:], nb)
-        load_scales([nc.sync] * 4, w1s, w1_scales)
+        load_live_rows(w1_raw_plane, w1_scales)
 
-        d1w = deal_words("d1w", w1w)
-        nc.vector.tensor_copy(xsg[:], xs[:].indirect(offs_sb[:]))
-        d1s = deal_plane("d1s", w1s)
-        for c in range(2):
-            nc.vector.tensor_copy(xwg[:, c * HALF : (c + 1) * HALF], xw[:].indirect(offs_sb[:, c * HALF // 16 : (c + 1) * HALF // 16]))
+        w1_dealt = deal_words("w1_dealt", w1_raw)
+        nc.vector.tensor_copy(x_plane[:], x_table_plane[:].indirect(offs_sb[:]))
+        w1_plane = deal_plane("w1_plane", w1_raw_plane)
+        for picked, cols in zip(x_picked, HALVES):
+            nc.vector.tensor_copy(picked[:], x_table[:].indirect(entries(offs_sb, cols)))
 
-        f0_rows = f0.rearrange("(p t) j -> p t j", t=PACK)
-        f0_sb = lap.tile([P, PACK, S], F32, name="f0_sb", offset=0, align_bytes=64)
+        f0_rows = f0.rearrange("(p t) j -> p t j", t=SLOTS)
+        f0_sb = reused.tile([P, SLOTS, S], F32, name="f0_sb", offset=F0_AT, align_bytes=64)
         nc.sync.dma_start(out=f0_sb[:, 0, :], in_=f0_rows[:, 0, :])
-        dr_sb = lap.tile([P, PACK], F32, name="dr_sb", offset=8192, align_bytes=64)
-        unit_sb = lap.tile([P, PACK], F32, name="unit_sb", offset=8256, align_bytes=64)
-        nc.sync.dma_start(out=dr_sb[:], in_=dr.rearrange("(p t) o -> p (t o)", t=PACK))
-        w2w = lap.tile([P, 2 * H], U8, name="w2w", offset=8320, align_bytes=64)
-        nc.sync.dma_start(out=w2w[:].bitcast(I32), in_=w2_words[0].bitcast(I32))
-        for t in range(1, PACK):
+        dr_sb = reused.tile([P, SLOTS], F32, name="dr_sb", offset=DR_AT, align_bytes=64)
+        unit_sb = reused.tile([P, SLOTS], F32, name="unit_sb", offset=UNIT_AT, align_bytes=64)
+        nc.sync.dma_start(out=dr_sb[:], in_=dr.rearrange("(p t) o -> p (t o)", t=SLOTS))
+        w2_raw = reused.tile([P, 2 * H], U8, name="w2_raw", offset=W2_WORDS_AT, align_bytes=64)
+        nc.sync.dma_start(out=w2_raw[:].bitcast(I32), in_=w2_words[0].bitcast(I32))
+        for t in range(1, SLOTS):
             nc.sync.dma_start(out=f0_sb[:, t, :], in_=f0_rows[:, t, :])
-        nc.sync.dma_start(out=unit_sb[:], in_=unit.rearrange("(p t) o -> p (t o)", t=PACK))
-        w2s = w1s
-        load_scales([nc.sync] * 4, w2s, w2_scales)
-        d2w = deal_words("d2w", w2w)
-        d2s = deal_plane("d2s", w2s)
-        w3w = lap.tile([P, 2 * N], U8, name="w3w", offset=8320, align_bytes=64)
-        w3s = w1s[:, 0:N]
-        nc.sync.dma_start(out=w3w[:].bitcast(I32), in_=w3_words[0].bitcast(I32))
-        load_scales([nc.sync] * 4, w3s, w3_scales)
+        nc.sync.dma_start(out=unit_sb[:], in_=unit.rearrange("(p t) o -> p (t o)", t=SLOTS))
+        late_plane = reused.tile([P, H], U8, name="late_plane", offset=LATE_PLANE_AT, align_bytes=64)
+        nc.vector.memset(late_plane[:].bitcast(I32), 0)
+        load_live_rows(late_plane, w2_scales)
+        w2_dealt = deal_words("w2_dealt", w2_raw)
+        w2_plane = deal_plane("w2_plane", late_plane)
+        w3_sb = reused.tile([P, 2 * N], U8, name="w3_sb", offset=W2_WORDS_AT, align_bytes=64)
+        w3_plane = late_plane[:, 0:N]
+        nc.sync.dma_start(out=w3_sb[:].bitcast(I32), in_=w3_words[0].bitcast(I32))
+        load_live_rows(w3_plane, w3_scales)
 
-        def product(bank, dw, ds, t, cols):
+        def product(bank, dealt, plane, t, cols):
             acc = psum.tile([P, cols.stop - cols.start], F32, name="acc", tag="bank%d" % bank)
-            nc.tensor.matmul_mx(out=acc[:], lhsT=dw[:, t, :].bitcast(FP4X4), lhsT_scale=ds[:, t, :], rhs=xwg[:, cols].bitcast(FP8X4), rhs_scale=xsg[:, cols], start=True, stop=True)
+            for lo in range(cols.start, cols.stop, HALF):
+                nc.tensor.matmul_mx(out=acc[:, lo - cols.start : lo - cols.start + HALF], lhsT=dealt[:, t, :].bitcast(FP4X4), lhsT_scale=plane[:, t, :], rhs=x_picked[lo // HALF][:].bitcast(FP8X4), rhs_scale=x_plane[:, lo : lo + HALF], start=True, stop=True)
             return acc
 
-        neg_freq = [keep.tile([P, S], F32, name="neg_freq%d" % t) for t in range(PACK)]
-        volt = [keep.tile([P, S], F32, name="volt%d" % t) for t in range(PACK)]
-        hid = keep.tile([P, PACK, S], BF16, name="hid", align_bytes=64)
-        gn = keep.tile([P, PACK, S], F32, name="gn")
-        slip = keep.tile([P, PACK, S], F32, name="slip")
-        th = keep.tile([P, PACK, S], F32, name="th")
-        pf = keep.tile([P, PACK, S], F32, name="pf")
-        qq = keep.tile([P, PACK, S], F32, name="qq")
-        aa = keep.tile([P, PACK, S], F32, name="aa")
-        bb = keep.tile([P, PACK, S], F32, name="bb")
-        vn = keep.tile([P, PACK, S], F32, name="vn")
-        WHOLE = slice(0, S)
-
-        def entries(cols):
-            return nb_sb[:, cols.start // 16 : cols.stop // 16]
+        neg_freq = [keep.tile([P, S], F32, name="neg_freq%d" % t) for t in range(SLOTS)]
+        volt = [keep.tile([P, S], F32, name="volt%d" % t) for t in range(SLOTS)]
+        hid = keep.tile([P, SLOTS, S], BF16, name="hid", align_bytes=64)
+        neg_freq_nb = keep.tile([P, SLOTS, S], F32, name="neg_freq_nb")
+        slip = keep.tile([P, SLOTS, S], F32, name="slip")
+        neg_tanh_slip = keep.tile([P, SLOTS, S], F32, name="neg_tanh_slip")
+        pull = keep.tile([P, SLOTS, S], F32, name="pull")
+        pull_nb = keep.tile([P, SLOTS, S], F32, name="pull_nb")
+        tanh_vt = keep.tile([P, SLOTS, S], F32, name="tanh_vt")
+        tanh_pw = keep.tile([P, SLOTS, S], F32, name="tanh_pw")
+        volt_nb = keep.tile([P, SLOTS, S], F32, name="volt_nb")
 
         def pieces(cols):
-            return [cols] if cols.stop - cols.start < S else [slice(0, HALF), slice(HALF, S)]
+            return HALVES if cols.stop - cols.start == S else (cols,)
 
         def frequency(t, bank, cols):
-            pw = product(bank, d1w, d1s, t, cols)
-            nc.scalar.activation(bb[:, t, cols], pw[:], ACT.Tanh)
-            nc.vector.scalar_tensor_tensor(neg_freq[t][:, cols], bb[:, t, cols], dr_sb[:, t : t + 1], f0_sb[:, t, cols], ALU.mult, ALU.subtract)
+            pw = product(bank, w1_dealt, w1_plane, t, cols)
+            nc.scalar.activation(tanh_pw[:, t, cols], pw[:], ACT.Tanh)
+            nc.vector.scalar_tensor_tensor(neg_freq[t][:, cols], tanh_pw[:, t, cols], dr_sb[:, t : t + 1], f0_sb[:, t, cols], ALU.mult, ALU.subtract)
 
         def voltage(t, bank):
-            vt = product(bank, d2w, d2s, t, WHOLE)
-            nc.scalar.activation(aa[:, t, :], vt[:], ACT.Tanh)
-            if t < 2:
-                nc.vector.tensor_scalar(volt[t][:], aa[:, t, :], 0.3, 1.0, ALU.mult, ALU.add)
+            vt = product(bank, w2_dealt, w2_plane, t, WHOLE)
+            nc.scalar.activation(tanh_vt[:, t, :], vt[:], ACT.Tanh)
+            if t < VOLTS_ON_VECTOR:
+                nc.vector.tensor_scalar(volt[t][:], tanh_vt[:, t, :], 0.3, 1.0, ALU.mult, ALU.add)
             else:
-                nc.scalar.activation(volt[t][:], aa[:, t, :], ACT.Copy, bias=1.0, scale=0.3)
+                nc.scalar.activation(volt[t][:], tanh_vt[:, t, :], ACT.Copy, bias=1.0, scale=0.3)
 
-        def fetch(dst, window, cols, on_scalar):
-            for part in pieces(cols):
-                if on_scalar:
-                    nc.scalar.activation(dst[:, part], window[:].indirect(entries(part)), ACT.Copy)
+        def slips(t):
+            for part in HALVES:
+                looked_up = neg_freq[t][:].indirect(entries(nb_sb, part))
+                if t < FREQ_GATHERS_ON_VECTOR:
+                    nc.vector.tensor_copy(neg_freq_nb[:, t, part], looked_up)
                 else:
-                    nc.vector.tensor_copy(dst[:, part], window[:].indirect(entries(part)))
-
-        def slips(t, cols):
-            fetch(gn[:, t, :], neg_freq[t], cols, t >= 1)
-            nc.vector.tensor_tensor(slip[:, t, cols], gn[:, t, cols], neg_freq[t][:, cols], ALU.subtract)
-            nc.scalar.activation(th[:, t, cols], slip[:, t, cols], ACT.Tanh, scale=-2.0)
+                    nc.scalar.activation(neg_freq_nb[:, t, part], looked_up, ACT.Copy)
+            nc.vector.tensor_tensor(slip[:, t, :], neg_freq_nb[:, t, :], neg_freq[t][:], ALU.subtract)
+            nc.scalar.activation(neg_tanh_slip[:, t, :], slip[:, t, :], ACT.Tanh, scale=-2.0)
 
         def hidden(t, cols):
-            nc.vector.scalar_tensor_tensor(pf[:, t, cols], th[:, t, cols], unit_sb[:, t : t + 1], neg_freq[t][:, cols], ALU.mult, ALU.mult)
-            if t >= 2:
-                fetch(vn[:, t, :], volt[t], cols, True)
-                nc.vector.tensor_tensor(qq[:, t, cols], vn[:, t, cols], pf[:, t, cols], ALU.mult)
-            else:
-                for part in pieces(cols):
-                    nc.vector.tensor_tensor(qq[:, t, part], volt[t][:].indirect(entries(part)), pf[:, t, part], ALU.mult)
-            nc.vector.scalar_tensor_tensor(hid[:, t, cols], qq[:, t, cols], unit_sb[:, t : t + 1], volt[t][:, cols], ALU.add, ALU.mult)
+            unit_t = unit_sb[:, t : t + 1]
+            nc.vector.scalar_tensor_tensor(pull[:, t, cols], neg_tanh_slip[:, t, cols], unit_t, neg_freq[t][:, cols], ALU.mult, ALU.mult)
+            for part in pieces(cols):
+                looked_up = volt[t][:].indirect(entries(nb_sb, part))
+                if t < VOLT_GATHERS_ON_VECTOR:
+                    nc.vector.tensor_tensor(pull_nb[:, t, part], looked_up, pull[:, t, part], ALU.mult)
+                else:
+                    nc.scalar.activation(volt_nb[:, t, part], looked_up, ACT.Copy)
+                    nc.vector.tensor_tensor(pull_nb[:, t, part], volt_nb[:, t, part], pull[:, t, part], ALU.mult)
+            nc.vector.scalar_tensor_tensor(hid[:, t, cols], pull_nb[:, t, cols], unit_t, volt[t][:, cols], ALU.add, ALU.mult)
 
         def feeders(c, cols):
             width = cols.stop - cols.start
-            woven = keep.tile([P, width, PACK], BF16, name="woven%d" % c, align_bytes=64)
+            woven = keep.tile([P, width, SLOTS], BF16, name="woven%d" % c, align_bytes=64)
             codes = keep.tile([P, width], U32, name="codes%d" % c, align_bytes=64)
-            plane = keep.tile([P, width], U8, name="plane%d" % c, align_bytes=64)
-            weave = nc.scalar.copy if c < 1 else nc.vector.tensor_copy
-            weave(out=woven[:].rearrange("p (g i) t -> p g t i", i=4), in_=hid[:, :, cols].rearrange("p t (g i) -> p g t i", i=4))
-            nc.vector.quantize_mx(out=codes[:].bitcast(FP8X4), scales=plane[:], in_=woven[:].rearrange("p j t -> p (j t)"))
-            acc = psum.tile([P, 2, width], F32, name="oacc", tag="bank%d" % (c + 1))
-            for h in range(2):
-                nc.tensor.matmul_mx(out=acc[:, h, :], lhsT=w3w[:, 2 * P * h : 2 * P * (h + 1)].bitcast(FP4X4), lhsT_scale=w3s[:, P * h : P * (h + 1)], rhs=codes[:].bitcast(FP8X4), rhs_scale=plane[:], start=True, stop=True)
-            res = keep.tile([P, 2, width], F32, name="res%d" % c)
-            nc.scalar.copy(res[:], acc[:])
-            nc.sync.dma_start(out=out.rearrange("(h m) j -> m h j", h=2)[:, :, cols], in_=res[:])
+            hid_plane = keep.tile([P, width], U8, name="hid_plane%d" % c, align_bytes=64)
+            weave = nc.scalar.copy if c < WEAVES_ON_SCALAR else nc.vector.tensor_copy
+            weave(out=woven[:].rearrange("p (g i) t -> p g t i", i=WEAVE_RUN), in_=hid[:, :, cols].rearrange("p t (g i) -> p g t i", i=WEAVE_RUN))
+            nc.vector.quantize_mx(out=codes[:].bitcast(FP8X4), scales=hid_plane[:], in_=woven[:].rearrange("p j t -> p (j t)"))
+            acc = psum.tile([P, N // P, width], F32, name="out_acc", tag="bank%d" % (c + 1))
+            for h in range(N // P):
+                nc.tensor.matmul_mx(out=acc[:, h, :], lhsT=w3_sb[:, 2 * P * h : 2 * P * (h + 1)].bitcast(FP4X4), lhsT_scale=w3_plane[:, P * h : P * (h + 1)], rhs=codes[:].bitcast(FP8X4), rhs_scale=hid_plane[:], start=True, stop=True)
+            result = keep.tile([P, N // P, width], F32, name="result%d" % c)
+            nc.scalar.copy(result[:], acc[:])
+            nc.sync.dma_start(out=out.rearrange("(h m) j -> m h j", h=N // P)[:, :, cols], in_=result[:])
 
-        frequency(0, 0, slice(0, HALF))
-        frequency(0, 1, slice(HALF, S))
-        for t in range(1, PACK):
+        for bank, cols in enumerate(HALVES):
+            frequency(0, bank, cols)
+        for t in range(1, SLOTS):
             frequency(t, t + 1, WHOLE)
-        for t in range(PACK):
-            slips(t, WHOLE)
-            voltage(t, (5 + t) % 8)
-        hidden(0, WHOLE)
-        hidden(1, WHOLE)
-        for c, (lo, hi) in enumerate(CHUNKS):
-            for t in (2, 3):
-                hidden(t, slice(lo, hi))
-            feeders(c, slice(lo, hi))
+        for t in range(SLOTS):
+            slips(t)
+            voltage(t, (SLOTS + 1 + t) % BANKS)
+        for t in range(SLOTS // 2):
+            hidden(t, WHOLE)
+        for c, cols in enumerate(CHUNKS):
+            for t in range(SLOTS // 2, SLOTS):
+                hidden(t, cols)
+            feeders(c, cols)

from contextlib import ExitStack

import concourse.mybir as mybir

K, T, S, N, H = 512, 2048, 512, 256, 512
FLOPS = 2 * K * H * S * 2 + 2 * H * N * S

F32 = mybir.dt.float32
BF16 = mybir.dt.bfloat16
I32 = mybir.dt.int32
U32 = mybir.dt.uint32
U16 = mybir.dt.uint16
U8 = mybir.dt.uint8
FP8X4 = mybir.dt.float8_e4m3fn_x4
FP4X4 = mybir.dt.float4_e2m1fn_x4
ALU = mybir.AluOpType
ACT = mybir.ActivationFunctionType

P = 128
SLOTS = 4
QUADS = 4
QUAD = P // QUADS
LIVE = 4
PER_COLUMN = 16
BANKS = 8
HALF = S // 2
WHOLE = slice(0, S)
HALVES = (slice(0, HALF), slice(HALF, S))

CHUNKS = (slice(0, 256), slice(256, 384), slice(384, 512))
WEAVE_RUN = 4

FREQ_GATHERS_ON_VECTOR = 1
VOLTS_ON_VECTOR = 2
VOLT_GATHERS_ON_VECTOR = 2
WEAVES_ON_SCALAR = 1

F0_AT = 0
DR_AT = F0_AT + SLOTS * S * 4
UNIT_AT = DR_AT + 64
LATE_PLANE_AT = UNIT_AT + 64
W2_WORDS_AT = LATE_PLANE_AT + H
W1_WORDS_AT = DR_AT - 64
W1_PLANE_AT = 10240


def tile_picked_ydroopc_flow_p_kernel(tc, x_words, x_scales, w1_words, w1_scales, w2_words, w2_scales, f0, dr, unit, w3_words, w3_scales, offs, nb, out):
    nc = tc.nc
    with ExitStack() as ctx:
        keep = ctx.enter_context(tc.tile_pool(name="keep", bufs=1))
        psum = ctx.enter_context(tc.psum_pool(name="psum", bufs=1))
        reused = ctx.enter_context(tc.tile_pool(name="reused", bufs=1))

        def load_live_rows(plane, scales):
            for q in range(QUADS):
                nc.sync.dma_start(out=plane[QUAD * q : QUAD * q + LIVE, :].bitcast(I32), in_=scales[0, LIVE * q : LIVE * (q + 1), :].bitcast(I32))

        def deal_words(name, words):
            dealt = keep.tile([P, SLOTS, 2 * P], U8, name=name, align_bytes=64)
            nc.vector.tensor_copy(out=dealt[:].rearrange("p t (m b) -> p t m b", b=2), in_=words[:].rearrange("p (m t b) -> p t m b", t=SLOTS, b=2))
            return dealt

        def deal_plane(name, plane):
            dealt = keep.tile([P, SLOTS, P], U8, name=name, align_bytes=64)
            nc.vector.tensor_copy(out=dealt[:], in_=plane[:].rearrange("p (m t) -> p t m", t=SLOTS))
            return dealt

        def entries(list_sb, cols):
            return list_sb[:, cols.start // PER_COLUMN : cols.stop // PER_COLUMN]

        offs_sb = keep.tile([P, S // PER_COLUMN], U16, name="offs_sb")
        nb_sb = keep.tile([P, S // PER_COLUMN], U16, name="nb_sb")
        x_table = keep.tile([P, T], U32, name="x_table", align_bytes=64)
        x_table_plane = keep.tile([P, T], U8, name="x_table_plane", align_bytes=64)
        w1_raw = reused.tile([P, 2 * H], U8, name="w1_raw", offset=W1_WORDS_AT, align_bytes=64)
        w1_raw_plane = reused.tile([P, H], U8, name="w1_raw_plane", offset=W1_PLANE_AT, align_bytes=64)
        x_plane = keep.tile([P, S], U8, name="x_plane", align_bytes=64)
        x_picked = [
            keep.tile([P, HALF], U32, name="x_picked0", align_bytes=64),
            reused.tile([P, HALF], U32, name="x_picked1", offset=W1_PLANE_AT, align_bytes=64),
        ]

        nc.vector.memset(w1_raw_plane[:].bitcast(I32), 0)

        nc.sync.dma_start(offs_sb[:], offs)
        nc.scalar.dma_start(out=w1_raw[:].bitcast(I32), in_=w1_words[0].bitcast(I32))
        for q in range(QUADS):
            rows = x_scales[0, LIVE * q : LIVE * (q + 1), :].bitcast(I32)
            queue = nc.sync if q < QUADS // 2 else nc.scalar
            queue.dma_start(out=x_table_plane[QUAD * q : QUAD * (q + 1), :].bitcast(I32), in_=rows.unsqueeze(0).to_broadcast([QUAD // LIVE, LIVE, T // 4]))
        nc.scalar.dma_start(out=x_table[:].bitcast(I32), in_=x_words[0].rearrange("p n t -> p (n t)").bitcast(I32))
        nc.sync.dma_start(nb_sb[:], nb)
        load_live_rows(w1_raw_plane, w1_scales)

        w1_dealt = deal_words("w1_dealt", w1_raw)
        nc.vector.tensor_copy(x_plane[:], x_table_plane[:].indirect(offs_sb[:]))
        w1_plane = deal_plane("w1_plane", w1_raw_plane)
        for picked, cols in zip(x_picked, HALVES):
            nc.vector.tensor_copy(picked[:], x_table[:].indirect(entries(offs_sb, cols)))

        f0_rows = f0.rearrange("(p t) j -> p t j", t=SLOTS)
        f0_sb = reused.tile([P, SLOTS, S], F32, name="f0_sb", offset=F0_AT, align_bytes=64)
        nc.sync.dma_start(out=f0_sb[:, 0, :], in_=f0_rows[:, 0, :])
        dr_sb = reused.tile([P, SLOTS], F32, name="dr_sb", offset=DR_AT, align_bytes=64)
        unit_sb = reused.tile([P, SLOTS], F32, name="unit_sb", offset=UNIT_AT, align_bytes=64)
        nc.sync.dma_start(out=dr_sb[:], in_=dr.rearrange("(p t) o -> p (t o)", t=SLOTS))
        w2_raw = reused.tile([P, 2 * H], U8, name="w2_raw", offset=W2_WORDS_AT, align_bytes=64)
        nc.sync.dma_start(out=w2_raw[:].bitcast(I32), in_=w2_words[0].bitcast(I32))
        for t in range(1, SLOTS):
            nc.sync.dma_start(out=f0_sb[:, t, :], in_=f0_rows[:, t, :])
        nc.sync.dma_start(out=unit_sb[:], in_=unit.rearrange("(p t) o -> p (t o)", t=SLOTS))
        late_plane = reused.tile([P, H], U8, name="late_plane", offset=LATE_PLANE_AT, align_bytes=64)
        nc.vector.memset(late_plane[:].bitcast(I32), 0)
        load_live_rows(late_plane, w2_scales)
        w2_dealt = deal_words("w2_dealt", w2_raw)
        w2_plane = deal_plane("w2_plane", late_plane)
        w3_sb = reused.tile([P, 2 * N], U8, name="w3_sb", offset=W2_WORDS_AT, align_bytes=64)
        w3_plane = late_plane[:, 0:N]
        nc.sync.dma_start(out=w3_sb[:].bitcast(I32), in_=w3_words[0].bitcast(I32))
        load_live_rows(w3_plane, w3_scales)

        def product(bank, dealt, plane, t, cols):
            acc = psum.tile([P, cols.stop - cols.start], F32, name="acc", tag="bank%d" % bank)
            for lo in range(cols.start, cols.stop, HALF):
                nc.tensor.matmul_mx(out=acc[:, lo - cols.start : lo - cols.start + HALF], lhsT=dealt[:, t, :].bitcast(FP4X4), lhsT_scale=plane[:, t, :], rhs=x_picked[lo // HALF][:].bitcast(FP8X4), rhs_scale=x_plane[:, lo : lo + HALF], start=True, stop=True)
            return acc

        neg_freq = [keep.tile([P, S], F32, name="neg_freq%d" % t) for t in range(SLOTS)]
        volt = [keep.tile([P, S], F32, name="volt%d" % t) for t in range(SLOTS)]
        hid = keep.tile([P, SLOTS, S], BF16, name="hid", align_bytes=64)
        neg_freq_nb = keep.tile([P, SLOTS, S], F32, name="neg_freq_nb")
        slip = keep.tile([P, SLOTS, S], F32, name="slip")
        neg_tanh_slip = keep.tile([P, SLOTS, S], F32, name="neg_tanh_slip")
        pull = keep.tile([P, SLOTS, S], F32, name="pull")
        pull_nb = keep.tile([P, SLOTS, S], F32, name="pull_nb")
        tanh_vt = keep.tile([P, SLOTS, S], F32, name="tanh_vt")
        tanh_pw = keep.tile([P, SLOTS, S], F32, name="tanh_pw")
        volt_nb = keep.tile([P, SLOTS, S], F32, name="volt_nb")

        def pieces(cols):
            return HALVES if cols.stop - cols.start == S else (cols,)

        def frequency(t, bank, cols):
            pw = product(bank, w1_dealt, w1_plane, t, cols)
            nc.scalar.activation(tanh_pw[:, t, cols], pw[:], ACT.Tanh)
            nc.vector.scalar_tensor_tensor(neg_freq[t][:, cols], tanh_pw[:, t, cols], dr_sb[:, t : t + 1], f0_sb[:, t, cols], ALU.mult, ALU.subtract)

        def voltage(t, bank):
            vt = product(bank, w2_dealt, w2_plane, t, WHOLE)
            nc.scalar.activation(tanh_vt[:, t, :], vt[:], ACT.Tanh)
            if t < VOLTS_ON_VECTOR:
                nc.vector.tensor_scalar(volt[t][:], tanh_vt[:, t, :], 0.3, 1.0, ALU.mult, ALU.add)
            else:
                nc.scalar.activation(volt[t][:], tanh_vt[:, t, :], ACT.Copy, bias=1.0, scale=0.3)

        def slips(t):
            for part in HALVES:
                looked_up = neg_freq[t][:].indirect(entries(nb_sb, part))
                if t < FREQ_GATHERS_ON_VECTOR:
                    nc.vector.tensor_copy(neg_freq_nb[:, t, part], looked_up)
                else:
                    nc.scalar.activation(neg_freq_nb[:, t, part], looked_up, ACT.Copy)
            nc.vector.tensor_tensor(slip[:, t, :], neg_freq_nb[:, t, :], neg_freq[t][:], ALU.subtract)
            nc.scalar.activation(neg_tanh_slip[:, t, :], slip[:, t, :], ACT.Tanh, scale=-2.0)

        def hidden(t, cols):
            unit_t = unit_sb[:, t : t + 1]
            nc.vector.scalar_tensor_tensor(pull[:, t, cols], neg_tanh_slip[:, t, cols], unit_t, neg_freq[t][:, cols], ALU.mult, ALU.mult)
            for part in pieces(cols):
                looked_up = volt[t][:].indirect(entries(nb_sb, part))
                if t < VOLT_GATHERS_ON_VECTOR:
                    nc.vector.tensor_tensor(pull_nb[:, t, part], looked_up, pull[:, t, part], ALU.mult)
                else:
                    nc.scalar.activation(volt_nb[:, t, part], looked_up, ACT.Copy)
                    nc.vector.tensor_tensor(pull_nb[:, t, part], volt_nb[:, t, part], pull[:, t, part], ALU.mult)
            nc.vector.scalar_tensor_tensor(hid[:, t, cols], pull_nb[:, t, cols], unit_t, volt[t][:, cols], ALU.add, ALU.mult)

        def feeders(c, cols):
            width = cols.stop - cols.start
            woven = keep.tile([P, width, SLOTS], BF16, name="woven%d" % c, align_bytes=64)
            codes = keep.tile([P, width], U32, name="codes%d" % c, align_bytes=64)
            hid_plane = keep.tile([P, width], U8, name="hid_plane%d" % c, align_bytes=64)
            weave = nc.scalar.copy if c < WEAVES_ON_SCALAR else nc.vector.tensor_copy
            weave(out=woven[:].rearrange("p (g i) t -> p g t i", i=WEAVE_RUN), in_=hid[:, :, cols].rearrange("p t (g i) -> p g t i", i=WEAVE_RUN))
            nc.vector.quantize_mx(out=codes[:].bitcast(FP8X4), scales=hid_plane[:], in_=woven[:].rearrange("p j t -> p (j t)"))
            acc = psum.tile([P, N // P, width], F32, name="out_acc", tag="bank%d" % (c + 1))
            for h in range(N // P):
                nc.tensor.matmul_mx(out=acc[:, h, :], lhsT=w3_sb[:, 2 * P * h : 2 * P * (h + 1)].bitcast(FP4X4), lhsT_scale=w3_plane[:, P * h : P * (h + 1)], rhs=codes[:].bitcast(FP8X4), rhs_scale=hid_plane[:], start=True, stop=True)
            result = keep.tile([P, N // P, width], F32, name="result%d" % c)
            nc.scalar.copy(result[:], acc[:])
            nc.sync.dma_start(out=out.rearrange("(h m) j -> m h j", h=N // P)[:, :, cols], in_=result[:])

        for bank, cols in enumerate(HALVES):
            frequency(0, bank, cols)
        for t in range(1, SLOTS):
            frequency(t, t + 1, WHOLE)
        for t in range(SLOTS):
            slips(t)
            voltage(t, (SLOTS + 1 + t) % BANKS)
        for t in range(SLOTS // 2):
            hidden(t, WHOLE)
        for c, cols in enumerate(CHUNKS):
            for t in range(SLOTS // 2, SLOTS):
                hidden(t, cols)
            feeders(c, cols)
